import numpy as np
import ml_dtypes


def mxq(x, axis, fmt="e4m3"):
    dtype, down = {"e4m3": (ml_dtypes.float8_e4m3fn, 7), "e5m2": (ml_dtypes.float8_e5m2, 14)}[fmt]
    v = np.moveaxis(np.asarray(x, np.float32).astype(ml_dtypes.bfloat16).astype(np.float64), axis, -1)
    blocks = v.reshape(v.shape[:-1] + (-1, 32))
    amax = np.abs(blocks).max(-1, keepdims=True)
    byte = np.maximum(np.where(amax > 0, np.frexp(amax)[1] - 1 + 127, 0) - down, 1)
    scale = np.exp2(byte - 127.0)
    codes = (blocks / scale).astype(np.float32).astype(dtype).astype(np.float64)
    return np.moveaxis((codes * scale).reshape(v.shape), -1, axis)


WIDE = False


def mx_kscale(k):
    if not WIDE:
        return np.ones(k)
    levels = np.array([30, -30])
    if k % 512:
        return np.exp2(np.random.permutation(np.resize(levels, k // 32))).repeat(32)
    a = np.empty((k // 512, 16))
    for p in range(k // 512):
        a[p, :8] = np.random.permutation(np.resize(levels, 8))
        for g in range(8):
            far = levels[np.abs(levels - a[p, g]) >= 10]
            a[p, g + 8] = far[np.random.randint(len(far))]
    return np.exp2(a.ravel()).repeat(32)


def f64(x):
    return np.asarray(x).astype(np.float64)


def striped(idx):
    return np.tile(np.asarray(idx).reshape(-1, 16).T, (8, 1)).astype(np.uint16)


def unstriped(offs):
    return offs[:16].T.reshape(-1).astype(np.int64)


E2M1 = np.array([0.0, 0.5, 1.0, 1.5, 2.0, 3.0, 4.0, 6.0, -0.0, -0.5, -1.0, -1.5, -2.0, -3.0, -4.0, -6.0])


def pack_weight(w, fmt):
    k, n = w.shape
    w = f64(np.asarray(w, np.float32).astype(ml_dtypes.bfloat16)).reshape(k // 32, 32, n)
    amax = np.abs(w).max(1)
    if fmt in ("e4m3", "e5m2"):
        byte = np.frexp(amax)[1] - 1 + 127 - (7 if fmt == "e4m3" else 14)
    else:
        mant, ex = np.frexp(amax / 6.0)
        byte = np.where(mant > 0.5, ex, ex - 1) + 127
    byte = np.clip(np.where(amax > 0, byte, 1), 1, 254)
    scaled = (w * np.exp2(127.0 - byte)[:, None, :]).reshape(k, n).astype(np.float32)
    by_word = np.ascontiguousarray(scaled.reshape(k // 512, 128, 4, n).transpose(0, 1, 3, 2))
    if fmt in ("e4m3", "e5m2"):
        words = by_word.astype(ml_dtypes.float8_e4m3fn if fmt == "e4m3" else ml_dtypes.float8_e5m2).view(np.uint8)
    else:
        c = by_word.astype(ml_dtypes.float4_e2m1fn).view(np.uint8) & 0xF
        words = (c[..., 0::2] | (c[..., 1::2] << 4)).reshape(k // 512, 128, 2 * n)
    return np.ascontiguousarray(words), np.ascontiguousarray(byte.astype(np.uint8).reshape(k // 512, 16, n))


def unpack_weight(words, scales, fmt):
    g, _, n = scales.shape
    words = np.ascontiguousarray(words).reshape(g, 128, n, -1)
    if fmt in ("e4m3", "e5m2"):
        vals = words.view(ml_dtypes.float8_e4m3fn if fmt == "e4m3" else ml_dtypes.float8_e5m2).astype(np.float64)
    else:
        nib = np.empty((g, 128, n, 4), np.uint8)
        nib[..., 0::2] = words & 0xF
        nib[..., 1::2] = words >> 4
        vals = E2M1[nib]
    vals = vals * np.repeat(np.exp2(scales.astype(np.float64) - 127.0), 8, axis=1)[..., None]
    return vals.transpose(0, 1, 3, 2).reshape(g * 512, n)


def sigmoid(v):
    return 1.0 / (1.0 + np.exp(-v))


K, F, T, Z, J, R, C, O, N, L, E = 512, 512, 1024, 1024, 256, 512, 512, 256, 256, 512, 1024


def setup_inputs():
    n = np.random.standard_normal
    idx = np.random.permutation(T)[:J]
    idx2 = np.random.permutation(Z)[:J]
    idx3 = np.random.permutation(C)[:J]
    idx4 = np.random.permutation(C)[:J]
    idx5 = np.random.permutation(C)[:O]
    idx6 = np.random.permutation(E)[:O]
    fk = mx_kscale(K)
    fr = mx_kscale(R)
    ff = mx_kscale(F)
    fl = mx_kscale(L)
    xtp = pack_weight(n((K, T)) / fk[:, None], "e5m2")
    wp = pack_weight(n((K, R)) * 1 / np.sqrt(K) * fk[:, None] * fr, "e2m1")
    xop = pack_weight(n((F, Z)) / ff[:, None], "e4m3")
    w2p = pack_weight(n((F, R)) * 1 / np.sqrt(F) * ff[:, None] * fr, "e2m1")
    wbp = pack_weight(n((R, N)) * 1 / np.sqrt(R) / fr[:, None], "e2m1")
    sxp = pack_weight(n((L, O)) / fl[:, None], "e4m3")
    wsp = pack_weight(n((L, N)) * 1 / np.sqrt(L) * fl[:, None], "e2m1")
    return {
        "xt_words": xtp[0],
        "xt_scales": xtp[1],
        "w_words": wp[0],
        "w_scales": wp[1],
        "xo_words": xop[0],
        "xo_scales": xop[1],
        "w2_words": w2p[0],
        "w2_scales": w2p[1],
        "wb_words": wbp[0],
        "wb_scales": wbp[1],
        "sx_words": sxp[0],
        "sx_scales": sxp[1],
        "ws_words": wsp[0],
        "ws_scales": wsp[1],
        "tz": (n((N, E))).astype(np.float32),
        "so": (np.random.uniform(0.6, 1.6, (N, 1))).astype(np.float32),
        "bo": (np.random.uniform(-1.0, 1.0, (N, 1))).astype(np.float32),
        "offs": striped(idx),
        "offs2": striped(idx2),
        "offs3": striped(idx3),
        "offs4": striped(idx4),
        "offs5": striped(idx5),
        "offs6": striped(idx6),
    }


def reference(xt_words, xt_scales, w_words, w_scales, xo_words, xo_scales, w2_words, w2_scales, wb_words, wb_scales, sx_words, sx_scales, ws_words, ws_scales, tz, so, bo, offs, offs2, offs3, offs4, offs5, offs6):
    idx = unstriped(offs)
    idx2 = unstriped(offs2)
    idx3 = unstriped(offs3)
    idx4 = unstriped(offs4)
    idx5 = unstriped(offs5)
    idx6 = unstriped(offs6)
    xtu = unpack_weight(xt_words, xt_scales, "e5m2")
    wu = unpack_weight(w_words, w_scales, "e2m1")
    xou = unpack_weight(xo_words, xo_scales, "e4m3")
    w2u = unpack_weight(w2_words, w2_scales, "e2m1")
    wbu = unpack_weight(wb_words, wb_scales, "e2m1")
    sxu = unpack_weight(sx_words, sx_scales, "e4m3")
    wsu = unpack_weight(ws_words, ws_scales, "e2m1")
    xtidxg = xtu[:, idx]
    a = wu.T @ xtidxg
    xoidx2g = xou[:, idx2]
    b = w2u.T @ xoidx2g
    pw = np.zeros((R, C))
    pw[:, idx3] = a
    pv = np.zeros((R, C))
    pv[:, idx4] = b
    pg = pw + pv
    hid = pg[:, idx5]
    hidq = mxq(hid, 0, "e4m3")
    p = wbu.T @ hidq + wsu.T @ sxu
    y = p * sigmoid(f64(tz)[:, idx6] * f64(so) + f64(bo))
    return y

@@ -1,0 +1,211 @@
+from contextlib import ExitStack
+
+import concourse.mybir as mybir
+
+K, T, J, R, C, O, N, E = 512, 1024, 256, 512, 512, 256, 256, 1024
+FLOPS = 2 * (2 * K * R * J + 2 * R * N * O)
+
+F32 = mybir.dt.float32
+BF16 = mybir.dt.bfloat16
+I32 = mybir.dt.int32
+U32 = mybir.dt.uint32
+U16 = mybir.dt.uint16
+U8 = mybir.dt.uint8
+E4M3X4 = mybir.dt.float8_e4m3fn_x4
+E5M2X4 = mybir.dt.float8_e5m2_x4
+E2M1X4 = mybir.dt.float4_e2m1fn_x4
+ACT = mybir.ActivationFunctionType
+ALU = mybir.AluOpType
+
+P = 128
+PACK = 4
+QUADS = 4
+
+
+def tile_list_twotab_shared_skip_finalgate_kernel(
+    tc, xt_words, xt_scales, w_words, w_scales, xo_words, xo_scales, w2_words, w2_scales,
+    wb_words, wb_scales, sx_words, sx_scales, ws_words, ws_scales, tz, so, bo,
+    offs, offs2, offs3, offs4, offs5, offs6, out,
+):
+    nc = tc.nc
+    with ExitStack() as ctx:
+        lists = ctx.enter_context(tc.tile_pool(name="lists", bufs=1))
+        sb = ctx.enter_context(tc.tile_pool(name="sb", bufs=1))
+        psum = ctx.enter_context(tc.psum_pool(name="psum", bufs=1))
+
+        def load_list(src, name):
+            tile = lists.tile([P, J // 16], U16, name=name)
+            nc.sync.dma_start(tile[:], src)
+            return tile
+
+        def zeroed_plane(cols, name):
+            tile = sb.tile([P, cols], U8, name=name, align_bytes=64)
+            nc.gpsimd.memset(tile[:].bitcast(I32), 0)
+            return tile
+
+        def load_scales(plane, src):
+            for q in range(QUADS):
+                nc.sync.dma_start(plane[32 * q : 32 * q + 4, :].bitcast(I32), src[0, 4 * q : 4 * q + 4, :].bitcast(I32))
+
+        def load_fp8_words(src, cols, name):
+            tile = sb.tile([P, cols], U32, name=name, align_bytes=64)
+            nc.sync.dma_start(tile[:].bitcast(I32), src[0].rearrange("p n t -> p (n t)").bitcast(I32))
+            return tile
+
+        def load_fp4_words(src, cols, name):
+            tile = sb.tile([P, 2 * cols], U8, name=name, align_bytes=64)
+            nc.sync.dma_start(tile[:].bitcast(I32), src[0].bitcast(I32))
+            return tile
+
+        def deal(copy, dst, src, run):
+            copy(
+                out=dst.rearrange("p (t h l) -> p h t l", t=PACK, l=run),
+                in_=src.rearrange("p (h l t) -> p h t l", t=PACK, l=run),
+            )
+
+        w_plane = zeroed_plane(R, "w_plane")
+        xt_plane = zeroed_plane(T, "xt_plane")
+        w2_plane = zeroed_plane(R, "w2_plane")
+        xo_plane = zeroed_plane(T, "xo_plane")
+        late_planes = zeroed_plane(2 * N + O, "late_planes")
+        ws_plane, wb_plane, sx_plane = late_planes[:, 0:N], late_planes[:, N : 2 * N], late_planes[:, 2 * N :]
+
+        list1 = load_list(offs, "list1")
+        load_scales(w_plane, w_scales)
+        w_sb = load_fp4_words(w_words, R, "w_sb")
+        xt_sb = load_fp8_words(xt_words, T, "xt_sb")
+        load_scales(xt_plane, xt_scales)
+        list3 = load_list(offs3, "list3")
+        list2 = load_list(offs2, "list2")
+        load_scales(w2_plane, w2_scales)
+        w2_sb = load_fp4_words(w2_words, R, "w2_sb")
+        xo_sb = load_fp8_words(xo_words, T, "xo_sb")
+        load_scales(xo_plane, xo_scales)
+        list4 = load_list(offs4, "list4")
+        list5 = load_list(offs5, "list5")
+        load_scales(ws_plane, ws_scales)
+        load_scales(sx_plane, sx_scales)
+        load_scales(wb_plane, wb_scales)
+        ws_sb = load_fp4_words(ws_words, N, "ws_sb")
+        sx_sb = load_fp8_words(sx_words, O, "sx_sb")
+        wb_sb = load_fp4_words(wb_words, N, "wb_sb")
+        list6 = load_list(offs6, "list6")
+        slope = sb.tile([P, N // P], F32, name="slope")
+        offset = sb.tile([P, N // P], F32, name="offset")
+        with nc.allow_non_contiguous_dma(reason="one value a partition"):
+            nc.sync.dma_start(slope[:], so.rearrange("(h p) one -> p (h one)", p=P))
+            nc.sync.dma_start(offset[:], bo.rearrange("(h p) one -> p (h one)", p=P))
+        tz_sb = [sb.tile([P, E], F32, name="tz_sb%d" % h) for h in range(N // P)]
+        for h in range(N // P):
+            nc.sync.dma_start(tz_sb[h][:], tz[P * h : P * (h + 1), :])
+
+        pw = [sb.tile([P, C], F32, name="pw%d" % t) for t in range(2)]
+        pv = [sb.tile([P, C], F32, name="pv%d" % t) for t in range(2)]
+        for page in pw + pv:
+            nc.vector.memset(page[:], 0.0)
+
+        def first_stage(name, words, plane, table, table_plane, picks, fmt, plane_copy):
+            dealt_plane = sb.tile([P, R], U8, name=name + "_dealt_plane", align_bytes=64)
+            deal(plane_copy, dealt_plane[:], plane[:], 16)
+            dealt = sb.tile([P, 2 * R], U8, name=name + "_dealt", align_bytes=64)
+            deal(nc.scalar.copy, dealt[:].bitcast(U16), words[:].bitcast(U16), 8)
+            got_plane = sb.tile([P, J], U8, name=name + "_got_plane", align_bytes=64)
+            nc.vector.tensor_copy(out=got_plane[:], in_=table_plane[:].indirect(picks[:]))
+            got = sb.tile([P, J], U32, name=name + "_got", align_bytes=64)
+            nc.vector.tensor_copy(out=got[:], in_=table[:].indirect(picks[:]))
+            banks = [psum.tile([P, 2 * J], F32, name="%s_bank%d" % (name, i)) for i in range(2)]
+            for t in range(PACK):
+                nc.tensor.matmul_mx(
+                    out=banks[t // 2][:, J * (t % 2) : J * (t % 2 + 1)],
+                    lhsT=dealt[:, 2 * P * t : 2 * P * (t + 1)].bitcast(E2M1X4),
+                    lhsT_scale=dealt_plane[:, P * t : P * (t + 1)],
+                    rhs=got[:].bitcast(fmt),
+                    rhs_scale=got_plane[:],
+                    start=True,
+                    stop=True,
+                )
+            return banks
+
+        def evacuate(bank, name):
+            tile = sb.tile([P, 2 * J], F32, name=name, tag=name)
+            nc.scalar.copy(out=tile[:], in_=bank[:])
+            return tile
+
+        def put(engine, page, places, pair, t):
+            values = pair[t // 2][:, J * (t % 2) : J * (t % 2 + 1)]
+            if engine == "scalar":
+                nc.scalar.activation(out=page[t % 2][:].indirect(places[:]), in_=values, func=ACT.Copy)
+            else:
+                nc.vector.tensor_copy(out=page[t % 2][:].indirect(places[:]), in_=values)
+
+        pg = [sb.tile([P, C], F32, name="pg%d" % t) for t in range(PACK)]
+        hid = sb.tile([P, O, PACK], BF16, name="hid", align_bytes=64)
+
+        def join(t):
+            nc.vector.tensor_tensor(out=pg[t][:], in0=pw[t % 2][:], in1=pv[t % 2][:], op=ALU.add)
+
+        def read(t):
+            nc.vector.tensor_copy(out=hid[:, :, t], in_=pg[t][:].indirect(list5[:]))
+
+        a_banks = first_stage("a", w_sb, w_plane, xt_sb, xt_plane, list1, E5M2X4, nc.vector.tensor_copy)
+        a_sb = [evacuate(a_banks[i], "a_sb%d" % i) for i in range(2)]
+        put("scalar", pw, list3, a_sb, 0)
+        b_banks = first_stage("b", w2_sb, w2_plane, xo_sb, xo_plane, list2, E4M3X4, nc.gpsimd.tensor_copy)
+        put("vector", pw, list3, a_sb, 1)
+        b_sb = [evacuate(b_banks[i], "b_sb%d" % i) for i in range(2)]
+
+        p_banks = [psum.tile([P, O], F32, name="p_bank%d" % h) for h in range(N // P)]
+        for h in range(N // P):
+            nc.tensor.matmul_mx(
+                out=p_banks[h][:],
+                lhsT=ws_sb[:, 2 * P * h : 2 * P * (h + 1)].bitcast(E2M1X4),
+                lhsT_scale=ws_plane[:, P * h : P * (h + 1)],
+                rhs=sx_sb[:].bitcast(E4M3X4),
+                rhs_scale=sx_plane,
+                start=True,
+                stop=False,
+            )
+
+        put("vector", pv, list4, b_sb, 0)
+        put("scalar", pv, list4, b_sb, 1)
+        join(0)
+        put("scalar", pw, list3, a_sb, 2)
+        join(1)
+        put("vector", pv, list4, b_sb, 2)
+        put("scalar", pw, list3, a_sb, 3)
+        read(0)
+        join(2)
+        put("scalar", pv, list4, b_sb, 3)
+        read(1)
+        read(2)
+        join(3)
+        read(3)
+
+        gate = sb.tile([P, 2 * O], F32, name="gate", tag="b_sb1")
+        for h in range(N // P):
+            nc.scalar.activation(
+                out=gate[:, O * h : O * (h + 1)],
+                in_=tz_sb[h][:].indirect(list6[:]),
+                func=ACT.Sigmoid,
+                bias=offset[:, h : h + 1],
+                scale=slope[:, h : h + 1],
+            )
+
+        hid_words = sb.tile([P, O], U32, name="hid_words", align_bytes=64)
+        hid_plane = sb.tile([P, O], U8, name="hid_plane", align_bytes=64)
+        nc.vector.quantize_mx(
+            out=hid_words[:].bitcast(E4M3X4), scales=hid_plane[:], in_=hid[:].rearrange("p o t -> p (o t)")
+        )
+        for h in range(N // P):
+            nc.tensor.matmul_mx(
+                out=p_banks[h][:],
+                lhsT=wb_sb[:, 2 * P * h : 2 * P * (h + 1)].bitcast(E2M1X4),
+                lhsT_scale=wb_plane[:, P * h : P * (h + 1)],
+                rhs=hid_words[:].bitcast(E4M3X4),
+                rhs_scale=hid_plane[:],
+                start=False,
+                stop=True,
+            )
+            result = sb.tile([P, O], F32, name="result%d" % h)
+            nc.vector.tensor_tensor(out=result[:], in0=p_banks[h][:], in1=gate[:, O * h : O * (h + 1)], op=ALU.mult)
+            nc.sync.dma_start(out[P * h : P * (h + 1), :], result[:])

@@ -38,23 +38,23 @@ def tile_list_twotab_shared_skip_finalgate_kernel(
             nc.sync.dma_start(tile[:], src)
             return tile
 
-        def zeroed_plane(cols, name):
-            tile = sb.tile([P, cols], U8, name=name, align_bytes=64)
-            nc.gpsimd.memset(tile[:].bitcast(I32), 0)
+        def zeroed_plane(cols, name, engine=nc.vector):
+            tile = sb.tile([P, cols], U8, name=name, tag=name, align_bytes=64)
+            engine.memset(tile[:].bitcast(I32), 0)
             return tile
 
-        def load_scales(plane, src):
+        def load_scales(plane, src, queue=nc.sync):
             for q in range(QUADS):
-                nc.sync.dma_start(plane[32 * q : 32 * q + 4, :].bitcast(I32), src[0, 4 * q : 4 * q + 4, :].bitcast(I32))
+                queue.dma_start(plane[32 * q : 32 * q + 4, :].bitcast(I32), src[0, 4 * q : 4 * q + 4, :].bitcast(I32))
 
-        def load_fp8_words(src, cols, name):
+        def load_fp8_words(src, cols, name, queue=nc.sync):
             tile = sb.tile([P, cols], U32, name=name, align_bytes=64)
-            nc.sync.dma_start(tile[:].bitcast(I32), src[0].rearrange("p n t -> p (n t)").bitcast(I32))
+            queue.dma_start(tile[:].bitcast(I32), src[0].rearrange("p n t -> p (n t)").bitcast(I32))
             return tile
 
-        def load_fp4_words(src, cols, name):
+        def load_fp4_words(src, cols, name, queue=nc.sync):
             tile = sb.tile([P, 2 * cols], U8, name=name, align_bytes=64)
-            nc.sync.dma_start(tile[:].bitcast(I32), src[0].bitcast(I32))
+            queue.dma_start(tile[:].bitcast(I32), src[0].bitcast(I32))
             return tile
 
         def deal(copy, dst, src, run):
@@ -63,24 +63,26 @@ def tile_list_twotab_shared_skip_finalgate_kernel(
                 in_=src.rearrange("p (h l t) -> p h t l", t=PACK, l=run),
             )
 
+        xt_plane = sb.tile([P, T], U8, name="xt_plane", align_bytes=64)
+        nc.vector.memset(xt_plane[:, : T // 2].bitcast(I32), 0)
+        nc.gpsimd.memset(xt_plane[:, T // 2 :].bitcast(I32), 0)
         w_plane = zeroed_plane(R, "w_plane")
-        xt_plane = zeroed_plane(T, "xt_plane")
-        w2_plane = zeroed_plane(R, "w2_plane")
+        w2_plane = zeroed_plane(R, "w2_plane", nc.gpsimd)
         xo_plane = zeroed_plane(T, "xo_plane")
-        late_planes = zeroed_plane(2 * N + O, "late_planes")
+        late_planes = zeroed_plane(2 * N + O, "late_planes", nc.gpsimd)
         ws_plane, wb_plane, sx_plane = late_planes[:, 0:N], late_planes[:, N : 2 * N], late_planes[:, 2 * N :]
 
         list1 = load_list(offs, "list1")
-        load_scales(w_plane, w_scales)
         w_sb = load_fp4_words(w_words, R, "w_sb")
-        xt_sb = load_fp8_words(xt_words, T, "xt_sb")
-        load_scales(xt_plane, xt_scales)
         list3 = load_list(offs3, "list3")
-        list2 = load_list(offs2, "list2")
-        load_scales(w2_plane, w2_scales)
-        w2_sb = load_fp4_words(w2_words, R, "w2_sb")
+        load_scales(xt_plane, xt_scales)
+        xt_sb = load_fp8_words(xt_words, T, "xt_sb")
+        load_scales(w_plane, w_scales)
         xo_sb = load_fp8_words(xo_words, T, "xo_sb")
+        list2 = load_list(offs2, "list2")
+        w2_sb = load_fp4_words(w2_words, R, "w2_sb")
         load_scales(xo_plane, xo_scales)
+        load_scales(w2_plane, w2_scales)
         list4 = load_list(offs4, "list4")
         list5 = load_list(offs5, "list5")
         load_scales(ws_plane, ws_scales)
@@ -99,60 +101,94 @@ def tile_list_twotab_shared_skip_finalgate_kernel(
         for h in range(N // P):
             nc.sync.dma_start(tz_sb[h][:], tz[P * h : P * (h + 1), :])
 
-        pw = [sb.tile([P, C], F32, name="pw%d" % t) for t in range(2)]
-        pv = [sb.tile([P, C], F32, name="pv%d" % t) for t in range(2)]
-        for page in pw + pv:
-            nc.vector.memset(page[:], 0.0)
+        pw = [sb.tile([P, C], F32, name="pw%d" % t) for t in range(PACK)]
+        pv = [sb.tile([P, C], F32, name="pv%d" % t) for t in range(PACK)]
 
-        def first_stage(name, words, plane, table, table_plane, picks, fmt, plane_copy):
-            dealt_plane = sb.tile([P, R], U8, name=name + "_dealt_plane", align_bytes=64)
-            deal(plane_copy, dealt_plane[:], plane[:], 16)
-            dealt = sb.tile([P, 2 * R], U8, name=name + "_dealt", align_bytes=64)
+        def deal_words(words, name):
+            dealt = sb.tile([P, 2 * R], U8, name=name, align_bytes=64)
             deal(nc.scalar.copy, dealt[:].bitcast(U16), words[:].bitcast(U16), 8)
-            got_plane = sb.tile([P, J], U8, name=name + "_got_plane", align_bytes=64)
-            nc.vector.tensor_copy(out=got_plane[:], in_=table_plane[:].indirect(picks[:]))
-            got = sb.tile([P, J], U32, name=name + "_got", align_bytes=64)
+            return dealt
+
+        def deal_plane(copy, plane, name):
+            dealt = sb.tile([P, R], U8, name=name, align_bytes=64)
+            deal(copy, dealt[:], plane[:], 16)
+            return dealt
+
+        def pick(table, picks, dtype, name):
+            got = sb.tile([P, J], dtype, name=name, align_bytes=64)
             nc.vector.tensor_copy(out=got[:], in_=table[:].indirect(picks[:]))
-            banks = [psum.tile([P, 2 * J], F32, name="%s_bank%d" % (name, i)) for i in range(2)]
+            return got
+
+        def first_stage(sums, words, plane, got, got_plane, fmt):
             for t in range(PACK):
                 nc.tensor.matmul_mx(
-                    out=banks[t // 2][:, J * (t % 2) : J * (t % 2 + 1)],
-                    lhsT=dealt[:, 2 * P * t : 2 * P * (t + 1)].bitcast(E2M1X4),
-                    lhsT_scale=dealt_plane[:, P * t : P * (t + 1)],
+                    out=sums[t],
+                    lhsT=words[:, 2 * P * t : 2 * P * (t + 1)].bitcast(E2M1X4),
+                    lhsT_scale=plane[:, P * t : P * (t + 1)],
                     rhs=got[:].bitcast(fmt),
                     rhs_scale=got_plane[:],
                     start=True,
                     stop=True,
                 )
-            return banks
 
-        def evacuate(bank, name):
-            tile = sb.tile([P, 2 * J], F32, name=name, tag=name)
-            nc.scalar.copy(out=tile[:], in_=bank[:])
-            return tile
+        def put_scalar(page, places, values):
+            nc.scalar.activation(out=page[:].indirect(places[:]), in_=values, func=ACT.Copy)
 
-        def put(engine, page, places, pair, t):
-            values = pair[t // 2][:, J * (t % 2) : J * (t % 2 + 1)]
-            if engine == "scalar":
-                nc.scalar.activation(out=page[t % 2][:].indirect(places[:]), in_=values, func=ACT.Copy)
-            else:
-                nc.vector.tensor_copy(out=page[t % 2][:].indirect(places[:]), in_=values)
+        def put_vector(page, places, values):
+            nc.vector.tensor_copy(out=page[:].indirect(places[:]), in_=values)
 
-        pg = [sb.tile([P, C], F32, name="pg%d" % t) for t in range(PACK)]
+        pg = [sb.tile([P, C], F32, name="pg%d" % t, tag="pg%d" % t) for t in range(PACK)]
         hid = sb.tile([P, O, PACK], BF16, name="hid", align_bytes=64)
 
-        def join(t):
-            nc.vector.tensor_tensor(out=pg[t][:], in0=pw[t % 2][:], in1=pv[t % 2][:], op=ALU.add)
+        def join(engine, t):
+            engine.tensor_tensor(out=pg[t][:], in0=pw[t][:], in1=pv[t][:], op=ALU.add)
 
         def read(t):
             nc.vector.tensor_copy(out=hid[:, :, t], in_=pg[t][:].indirect(list5[:]))
 
-        a_banks = first_stage("a", w_sb, w_plane, xt_sb, xt_plane, list1, E5M2X4, nc.vector.tensor_copy)
-        a_sb = [evacuate(a_banks[i], "a_sb%d" % i) for i in range(2)]
-        put("scalar", pw, list3, a_sb, 0)
-        b_banks = first_stage("b", w2_sb, w2_plane, xo_sb, xo_plane, list2, E4M3X4, nc.gpsimd.tensor_copy)
-        put("vector", pw, list3, a_sb, 1)
-        b_sb = [evacuate(b_banks[i], "b_sb%d" % i) for i in range(2)]
+        w_dealt = deal_words(w_sb, "w_dealt")
+        xt_got_plane = pick(xt_plane, list1, U8, "xt_got_plane")
+        xt_got = pick(xt_sb, list1, U32, "xt_got")
+        w_dealt_plane = sb.tile([P, R], U8, name="w_dealt_plane", align_bytes=64)
+        for t in range(PACK):
+            nc.vector.tensor_copy(out=w_dealt_plane[:, P * t : P * (t + 1)], in_=w_plane[:, t::PACK])
+        a_banks = [psum.tile([P, J], F32, name="a_bank%d" % t) for t in range(PACK)]
+        first_stage([bank[:] for bank in a_banks], w_dealt, w_dealt_plane, xt_got, xt_got_plane, E5M2X4)
+        for page in pw:
+            nc.vector.memset(page[:].bitcast(I32), 0)
+        for page in pv:
+            nc.gpsimd.memset(page[:].bitcast(I32), 0)
+
+        a_sb = [sb.tile([P, J], F32, name="a_sb%d" % t) for t in range(2)]
+        nc.scalar.copy(out=a_sb[0][:], in_=a_banks[0][:])
+        nc.scalar.copy(out=a_sb[1][:], in_=a_banks[1][:])
+        put_scalar(pw[0], list3, a_sb[0][:])
+        put_scalar(pw[1], list3, a_sb[1][:])
+
+        xo_got = pick(xo_sb, list2, U32, "xo_got")
+        xo_got_plane = pick(xo_plane, list2, U8, "xo_got_plane")
+        w2_dealt = sb.tile([P, 2 * R], U8, name="w2_dealt", align_bytes=64)
+        nc.gpsimd.tensor_copy(
+            out=w2_dealt[:].rearrange("p (t h l b) -> p h t l b", t=PACK, l=8, b=2),
+            in_=w2_sb[:].rearrange("p (h l t b) -> p h t l b", t=PACK, l=8, b=2),
+        )
+        w2_dealt_plane = deal_plane(nc.gpsimd.tensor_copy, w2_plane, "w2_dealt_plane")
+        b_banks = [psum.tile([P, 2 * J], F32, name="b_bank%d" % i) for i in range(2)]
+        b_sums = [b_banks[t // 2][:, J * (t % 2) : J * (t % 2 + 1)] for t in range(PACK)]
+        first_stage(b_sums, w2_dealt, w2_dealt_plane, xo_got, xo_got_plane, E4M3X4)
+
+        a_late = sb.tile([P, 2, J], F32, name="a_late", tag="xo_plane", align_bytes=64)
+        for i in range(2):
+            nc.vector.tensor_copy(out=a_late[:, i, :], in_=a_banks[2 + i][:])
+        for i in range(2):
+            put_vector(pw[2 + i], list3, a_late[:, i, :])
+
+        b_sb = [sb.tile([P, 2 * J], F32, name="b_sb%d" % i, tag="b_sb%d" % i) for i in range(2)]
+        b_vals = [b_sb[t // 2][:, J * (t % 2) : J * (t % 2 + 1)] for t in range(PACK)]
+        nc.scalar.copy(out=b_sb[0][:], in_=b_banks[0][:])
+        nc.scalar.copy(out=b_sb[1][:], in_=b_banks[1][:])
+        put_scalar(pv[0], list4, b_vals[0])
+        put_vector(pv[1], list4, b_vals[1])
 
         p_banks = [psum.tile([P, O], F32, name="p_bank%d" % h) for h in range(N // P)]
         for h in range(N // P):
@@ -166,22 +202,20 @@ def tile_list_twotab_shared_skip_finalgate_kernel(
                 stop=False,
             )
 
-        put("vector", pv, list4, b_sb, 0)
-        put("scalar", pv, list4, b_sb, 1)
-        join(0)
-        put("scalar", pw, list3, a_sb, 2)
-        join(1)
-        put("vector", pv, list4, b_sb, 2)
-        put("scalar", pw, list3, a_sb, 3)
-        read(0)
-        join(2)
-        put("scalar", pv, list4, b_sb, 3)
-        read(1)
+        put_scalar(pv[2], list4, b_vals[2])
+        put_vector(pv[3], list4, b_vals[3])
+        join(nc.gpsimd, 0)
+        join(nc.gpsimd, 1)
+        join(nc.vector, 2)
+        join(nc.vector, 3)
+        hid_low = sb.tile([P, 2, O], BF16, name="hid_low")
+        for t in range(2):
+            nc.scalar.activation(out=hid_low[:, t, :], in_=pg[t][:].indirect(list5[:]), func=ACT.Copy)
         read(2)
-        join(3)
+        nc.vector.tensor_copy(out=hid[:, :, 0:2], in_=hid_low[:].rearrange("p t o -> p o t"))
         read(3)
 
-        gate = sb.tile([P, 2 * O], F32, name="gate", tag="b_sb1")
+        gate = sb.tile([P, 2 * O], F32, name="gate", tag="pg1")
         for h in range(N // P):
             nc.scalar.activation(
                 out=gate[:, O * h : O * (h + 1)],

from contextlib import ExitStack

import concourse.mybir as mybir

K, T, J, R, C, O, N, E = 512, 1024, 256, 512, 512, 256, 256, 1024
FLOPS = 2 * (2 * K * R * J + 2 * R * N * O)

F32 = mybir.dt.float32
BF16 = mybir.dt.bfloat16
I32 = mybir.dt.int32
U32 = mybir.dt.uint32
U16 = mybir.dt.uint16
U8 = mybir.dt.uint8
E4M3X4 = mybir.dt.float8_e4m3fn_x4
E5M2X4 = mybir.dt.float8_e5m2_x4
E2M1X4 = mybir.dt.float4_e2m1fn_x4
ACT = mybir.ActivationFunctionType
ALU = mybir.AluOpType

P = 128
PACK = 4
QUADS = 4


def tile_list_twotab_shared_skip_finalgate_kernel(
    tc, xt_words, xt_scales, w_words, w_scales, xo_words, xo_scales, w2_words, w2_scales,
    wb_words, wb_scales, sx_words, sx_scales, ws_words, ws_scales, tz, so, bo,
    offs, offs2, offs3, offs4, offs5, offs6, out,
):
    nc = tc.nc
    with ExitStack() as ctx:
        lists = ctx.enter_context(tc.tile_pool(name="lists", bufs=1))
        sb = ctx.enter_context(tc.tile_pool(name="sb", bufs=1))
        psum = ctx.enter_context(tc.psum_pool(name="psum", bufs=1))

        def load_list(src, name):
            tile = lists.tile([P, J // 16], U16, name=name)
            nc.sync.dma_start(tile[:], src)
            return tile

        def zeroed_plane(cols, name, engine=nc.vector):
            tile = sb.tile([P, cols], U8, name=name, tag=name, align_bytes=64)
            engine.memset(tile[:].bitcast(I32), 0)
            return tile

        def load_scales(plane, src, queue=nc.sync):
            for q in range(QUADS):
                queue.dma_start(plane[32 * q : 32 * q + 4, :].bitcast(I32), src[0, 4 * q : 4 * q + 4, :].bitcast(I32))

        def load_fp8_words(src, cols, name, queue=nc.sync):
            tile = sb.tile([P, cols], U32, name=name, align_bytes=64)
            queue.dma_start(tile[:].bitcast(I32), src[0].rearrange("p n t -> p (n t)").bitcast(I32))
            return tile

        def load_fp4_words(src, cols, name, queue=nc.sync):
            tile = sb.tile([P, 2 * cols], U8, name=name, align_bytes=64)
            queue.dma_start(tile[:].bitcast(I32), src[0].bitcast(I32))
            return tile

        def deal(copy, dst, src, run):
            copy(
                out=dst.rearrange("p (t h l) -> p h t l", t=PACK, l=run),
                in_=src.rearrange("p (h l t) -> p h t l", t=PACK, l=run),
            )

        xt_plane = sb.tile([P, T], U8, name="xt_plane", align_bytes=64)
        nc.vector.memset(xt_plane[:, : T // 2].bitcast(I32), 0)
        nc.gpsimd.memset(xt_plane[:, T // 2 :].bitcast(I32), 0)
        w_plane = zeroed_plane(R, "w_plane")
        w2_plane = zeroed_plane(R, "w2_plane", nc.gpsimd)
        xo_plane = zeroed_plane(T, "xo_plane")
        late_planes = zeroed_plane(2 * N + O, "late_planes", nc.gpsimd)
        ws_plane, wb_plane, sx_plane = late_planes[:, 0:N], late_planes[:, N : 2 * N], late_planes[:, 2 * N :]

        list1 = load_list(offs, "list1")
        w_sb = load_fp4_words(w_words, R, "w_sb")
        list3 = load_list(offs3, "list3")
        load_scales(xt_plane, xt_scales)
        xt_sb = load_fp8_words(xt_words, T, "xt_sb")
        load_scales(w_plane, w_scales)
        xo_sb = load_fp8_words(xo_words, T, "xo_sb")
        list2 = load_list(offs2, "list2")
        w2_sb = load_fp4_words(w2_words, R, "w2_sb")
        load_scales(xo_plane, xo_scales)
        load_scales(w2_plane, w2_scales)
        list4 = load_list(offs4, "list4")
        list5 = load_list(offs5, "list5")
        load_scales(ws_plane, ws_scales)
        load_scales(sx_plane, sx_scales)
        load_scales(wb_plane, wb_scales)
        ws_sb = load_fp4_words(ws_words, N, "ws_sb")
        sx_sb = load_fp8_words(sx_words, O, "sx_sb")
        wb_sb = load_fp4_words(wb_words, N, "wb_sb")
        list6 = load_list(offs6, "list6")
        slope = sb.tile([P, N // P], F32, name="slope")
        offset = sb.tile([P, N // P], F32, name="offset")
        with nc.allow_non_contiguous_dma(reason="one value a partition"):
            nc.sync.dma_start(slope[:], so.rearrange("(h p) one -> p (h one)", p=P))
            nc.sync.dma_start(offset[:], bo.rearrange("(h p) one -> p (h one)", p=P))
        tz_sb = [sb.tile([P, E], F32, name="tz_sb%d" % h) for h in range(N // P)]
        for h in range(N // P):
            nc.sync.dma_start(tz_sb[h][:], tz[P * h : P * (h + 1), :])

        pw = [sb.tile([P, C], F32, name="pw%d" % t) for t in range(PACK)]
        pv = [sb.tile([P, C], F32, name="pv%d" % t) for t in range(PACK)]

        def deal_words(words, name):
            dealt = sb.tile([P, 2 * R], U8, name=name, align_bytes=64)
            deal(nc.scalar.copy, dealt[:].bitcast(U16), words[:].bitcast(U16), 8)
            return dealt

        def deal_plane(copy, plane, name):
            dealt = sb.tile([P, R], U8, name=name, align_bytes=64)
            deal(copy, dealt[:], plane[:], 16)
            return dealt

        def pick(table, picks, dtype, name):
            got = sb.tile([P, J], dtype, name=name, align_bytes=64)
            nc.vector.tensor_copy(out=got[:], in_=table[:].indirect(picks[:]))
            return got

        def first_stage(sums, words, plane, got, got_plane, fmt):
            for t in range(PACK):
                nc.tensor.matmul_mx(
                    out=sums[t],
                    lhsT=words[:, 2 * P * t : 2 * P * (t + 1)].bitcast(E2M1X4),
                    lhsT_scale=plane[:, P * t : P * (t + 1)],
                    rhs=got[:].bitcast(fmt),
                    rhs_scale=got_plane[:],
                    start=True,
                    stop=True,
                )

        def put_scalar(page, places, values):
            nc.scalar.activation(out=page[:].indirect(places[:]), in_=values, func=ACT.Copy)

        def put_vector(page, places, values):
            nc.vector.tensor_copy(out=page[:].indirect(places[:]), in_=values)

        pg = [sb.tile([P, C], F32, name="pg%d" % t, tag="pg%d" % t) for t in range(PACK)]
        hid = sb.tile([P, O, PACK], BF16, name="hid", align_bytes=64)

        def join(engine, t):
            engine.tensor_tensor(out=pg[t][:], in0=pw[t][:], in1=pv[t][:], op=ALU.add)

        def read(t):
            nc.vector.tensor_copy(out=hid[:, :, t], in_=pg[t][:].indirect(list5[:]))

        w_dealt = deal_words(w_sb, "w_dealt")
        xt_got_plane = pick(xt_plane, list1, U8, "xt_got_plane")
        xt_got = pick(xt_sb, list1, U32, "xt_got")
        w_dealt_plane = sb.tile([P, R], U8, name="w_dealt_plane", align_bytes=64)
        for t in range(PACK):
            nc.vector.tensor_copy(out=w_dealt_plane[:, P * t : P * (t + 1)], in_=w_plane[:, t::PACK])
        a_banks = [psum.tile([P, J], F32, name="a_bank%d" % t) for t in range(PACK)]
        first_stage([bank[:] for bank in a_banks], w_dealt, w_dealt_plane, xt_got, xt_got_plane, E5M2X4)
        for page in pw:
            nc.vector.memset(page[:].bitcast(I32), 0)
        for page in pv:
            nc.gpsimd.memset(page[:].bitcast(I32), 0)

        a_sb = [sb.tile([P, J], F32, name="a_sb%d" % t) for t in range(2)]
        nc.scalar.copy(out=a_sb[0][:], in_=a_banks[0][:])
        nc.scalar.copy(out=a_sb[1][:], in_=a_banks[1][:])
        put_scalar(pw[0], list3, a_sb[0][:])
        put_scalar(pw[1], list3, a_sb[1][:])

        xo_got = pick(xo_sb, list2, U32, "xo_got")
        xo_got_plane = pick(xo_plane, list2, U8, "xo_got_plane")
        w2_dealt = sb.tile([P, 2 * R], U8, name="w2_dealt", align_bytes=64)
        nc.gpsimd.tensor_copy(
            out=w2_dealt[:].rearrange("p (t h l b) -> p h t l b", t=PACK, l=8, b=2),
            in_=w2_sb[:].rearrange("p (h l t b) -> p h t l b", t=PACK, l=8, b=2),
        )
        w2_dealt_plane = deal_plane(nc.gpsimd.tensor_copy, w2_plane, "w2_dealt_plane")
        b_banks = [psum.tile([P, 2 * J], F32, name="b_bank%d" % i) for i in range(2)]
        b_sums = [b_banks[t // 2][:, J * (t % 2) : J * (t % 2 + 1)] for t in range(PACK)]
        first_stage(b_sums, w2_dealt, w2_dealt_plane, xo_got, xo_got_plane, E4M3X4)

        a_late = sb.tile([P, 2, J], F32, name="a_late", tag="xo_plane", align_bytes=64)
        for i in range(2):
            nc.vector.tensor_copy(out=a_late[:, i, :], in_=a_banks[2 + i][:])
        for i in range(2):
            put_vector(pw[2 + i], list3, a_late[:, i, :])

        b_sb = [sb.tile([P, 2 * J], F32, name="b_sb%d" % i, tag="b_sb%d" % i) for i in range(2)]
        b_vals = [b_sb[t // 2][:, J * (t % 2) : J * (t % 2 + 1)] for t in range(PACK)]
        nc.scalar.copy(out=b_sb[0][:], in_=b_banks[0][:])
        nc.scalar.copy(out=b_sb[1][:], in_=b_banks[1][:])
        put_scalar(pv[0], list4, b_vals[0])
        put_vector(pv[1], list4, b_vals[1])

        p_banks = [psum.tile([P, O], F32, name="p_bank%d" % h) for h in range(N // P)]
        for h in range(N // P):
            nc.tensor.matmul_mx(
                out=p_banks[h][:],
                lhsT=ws_sb[:, 2 * P * h : 2 * P * (h + 1)].bitcast(E2M1X4),
                lhsT_scale=ws_plane[:, P * h : P * (h + 1)],
                rhs=sx_sb[:].bitcast(E4M3X4),
                rhs_scale=sx_plane,
                start=True,
                stop=False,
            )

        put_scalar(pv[2], list4, b_vals[2])
        put_vector(pv[3], list4, b_vals[3])
        join(nc.gpsimd, 0)
        join(nc.gpsimd, 1)
        join(nc.vector, 2)
        join(nc.vector, 3)
        hid_low = sb.tile([P, 2, O], BF16, name="hid_low")
        for t in range(2):
            nc.scalar.activation(out=hid_low[:, t, :], in_=pg[t][:].indirect(list5[:]), func=ACT.Copy)
        read(2)
        nc.vector.tensor_copy(out=hid[:, :, 0:2], in_=hid_low[:].rearrange("p t o -> p o t"))
        read(3)

        gate = sb.tile([P, 2 * O], F32, name="gate", tag="pg1")
        for h in range(N // P):
            nc.scalar.activation(
                out=gate[:, O * h : O * (h + 1)],
                in_=tz_sb[h][:].indirect(list6[:]),
                func=ACT.Sigmoid,
                bias=offset[:, h : h + 1],
                scale=slope[:, h : h + 1],
            )

        hid_words = sb.tile([P, O], U32, name="hid_words", align_bytes=64)
        hid_plane = sb.tile([P, O], U8, name="hid_plane", align_bytes=64)
        nc.vector.quantize_mx(
            out=hid_words[:].bitcast(E4M3X4), scales=hid_plane[:], in_=hid[:].rearrange("p o t -> p (o t)")
        )
        for h in range(N // P):
            nc.tensor.matmul_mx(
                out=p_banks[h][:],
                lhsT=wb_sb[:, 2 * P * h : 2 * P * (h + 1)].bitcast(E2M1X4),
                lhsT_scale=wb_plane[:, P * h : P * (h + 1)],
                rhs=hid_words[:].bitcast(E4M3X4),
                rhs_scale=hid_plane[:],
                start=False,
                stop=True,
            )
            result = sb.tile([P, O], F32, name="result%d" % h)
            nc.vector.tensor_tensor(out=result[:], in0=p_banks[h][:], in1=gate[:, O * h : O * (h + 1)], op=ALU.mult)
            nc.sync.dma_start(out[P * h : P * (h + 1), :], result[:])
